import numpy as np
import ml_dtypes


def mxq(x, axis, fmt="e4m3"):
    dtype, down = {"e4m3": (ml_dtypes.float8_e4m3fn, 7), "e5m2": (ml_dtypes.float8_e5m2, 14)}[fmt]
    v = np.moveaxis(np.asarray(x, np.float32).astype(ml_dtypes.bfloat16).astype(np.float64), axis, -1)
    blocks = v.reshape(v.shape[:-1] + (-1, 32))
    amax = np.abs(blocks).max(-1, keepdims=True)
    byte = np.maximum(np.where(amax > 0, np.frexp(amax)[1] - 1 + 127, 0) - down, 1)
    scale = np.exp2(byte - 127.0)
    codes = (blocks / scale).astype(np.float32).astype(dtype).astype(np.float64)
    return np.moveaxis((codes * scale).reshape(v.shape), -1, axis)


WIDE = False


def mx_kscale(k):
    if not WIDE:
        return np.ones(k)
    levels = np.array([10, -10, 5, -5, 0])
    if k % 512:
        return np.exp2(np.random.permutation(np.resize(levels, k // 32))).repeat(32)
    a = np.empty((k // 512, 16))
    for p in range(k // 512):
        a[p, :8] = np.random.permutation(np.resize(levels, 8))
        for g in range(8):
            far = levels[np.abs(levels - a[p, g]) >= 10]
            a[p, g + 8] = far[np.random.randint(len(far))]
    return np.exp2(a.ravel()).repeat(32)


def f64(x):
    return np.asarray(x).astype(np.float64)


def striped(idx):
    return np.tile(idx.reshape(-1, 16).T, (8, 1)).astype(np.uint16)


def unstriped(offs):
    return offs[:16].T.reshape(-1).astype(np.int64)


def striped8(idx):
    return np.concatenate([x.reshape(-1, 16).T for x in idx]).astype(np.uint16)


def runs(offs, k):
    lists = np.stack([offs[16 * r : 16 * r + 16].T.reshape(-1) for r in range(8)]).astype(np.int64)
    return lists[np.arange(k) % 512 // 64]


def pack_weight(w):
    k, n = w.shape
    w = f64(np.asarray(w, np.float32).astype(ml_dtypes.bfloat16)).reshape(k // 32, 32, n)
    amax = np.abs(w).max(1)
    byte = np.clip(np.where(amax > 0, np.frexp(amax)[1] - 1 + 127 - 7, 1), 1, 254)
    scaled = (w * np.exp2(127.0 - byte)[:, None, :]).reshape(k, n).astype(np.float32)
    words = np.ascontiguousarray(scaled.reshape(k // 512, 128, 4, n).transpose(0, 1, 3, 2)).astype(ml_dtypes.float8_e4m3fn).view(np.uint8)
    return words, np.ascontiguousarray(byte.astype(np.uint8).reshape(k // 512, 16, n))


def unpack_weight(words, scales):
    g, p, n, _ = words.shape
    vals = np.ascontiguousarray(words).view(ml_dtypes.float8_e4m3fn).astype(np.float64) * np.repeat(np.exp2(scales.astype(np.float64) - 127.0), 8, axis=1)[..., None]
    return vals.transpose(0, 1, 3, 2).reshape(g * 512, n)


def sigmoid(v):
    return 1.0 / (1.0 + np.exp(-np.maximum(v, -700.0)))

def planes(y):
    n, m = y.shape
    v = y.astype(np.float32).astype(ml_dtypes.bfloat16).astype(np.float64).reshape(n // 32, 32, m)
    top = np.abs(v).max(1)
    byte = np.clip(np.where(top > 0, np.frexp(top)[1] - 1 + 127 - 7, 1), 1, 254)
    codes = (v * np.exp2(127.0 - byte)[:, None, :]).reshape(n, m).astype(np.float32).astype(ml_dtypes.float8_e4m3fn).view(np.uint8)
    words = codes.reshape(n // 512, 128, 4, m).transpose(0, 1, 3, 2)
    return np.ascontiguousarray(words), np.ascontiguousarray(byte.astype(np.uint8).reshape(n // 512, 16, m))


K, T, S, N, H = 512, 2048, 512, 512, 512


def setup_inputs():
    n = np.random.standard_normal
    s = mx_kscale(K)[:, None]
    u = mx_kscale(S)
    packed_xT = pack_weight(n((K, T)) * s)
    return {
        "x_words": packed_xT[0],
        "x_scales": packed_xT[1],
        "wa": (n((K, H)) / np.sqrt(K) / s).astype(np.float32),
        "wb": (n((K, N)) / np.sqrt(K) / s).astype(np.float32),
        "gt": (np.random.uniform(0.5, 1.5, (S, 1)) * u[:, None]).astype(np.float32),
        "gi": (np.random.uniform(0.5, 1.5, (S, 1)) / u[:, None]).astype(np.float32),
        "offs": striped(np.random.permutation(T)[:S]),
        "two": striped(np.random.permutation(T)[:S]),
        "fa": striped8(np.stack([np.random.permutation(H) for _ in range(8)])),
        "fb": striped8(np.stack([np.random.permutation(N) for _ in range(8)])),
    }


def reference(x_words, x_scales, wa, wb, gt, gi, offs, two, fa, fb):
    xq = unpack_weight(x_words, x_scales)[:, unstriped(offs)]
    a = xq.T @ mxq(f64(wa), 0, "e4m3")
    z = f64(gt) * (a * (sigmoid(a[np.arange(S)[:, None], runs(fa, S)])))
    x_two = unpack_weight(x_words, x_scales)[:, unstriped(two)]
    b = x_two.T @ mxq(f64(wb), 0, "e4m3")
    z2 = f64(gi) * (b * (sigmoid(b[np.arange(S)[:, None], runs(fb, S)])))
    cv = 0.0625 * ((mxq(z, 0, "e4m3").T @ mxq(z2, 0, "e4m3")))
    out_0 = np.tanh(cv)
    return (out_0,) + planes(out_0)

@@ -1,0 +1,232 @@
+from contextlib import ExitStack
+
+import concourse.mybir as mybir
+from concourse.masks import make_identity
+
+F32 = mybir.dt.float32
+BF16 = mybir.dt.bfloat16
+I32 = mybir.dt.int32
+U32 = mybir.dt.uint32
+U16 = mybir.dt.uint16
+U8 = mybir.dt.uint8
+FP8X4 = mybir.dt.float8_e4m3fn_x4
+ACT = mybir.ActivationFunctionType
+MULT = mybir.AluOpType.mult
+
+P = 128
+PACK = 4
+T = 2048
+S = 512
+WIDTH = 512
+HALF = WIDTH // 2
+QUARTER = WIDTH // 4
+PER_COLUMN = 16
+BANK = 512
+CHUNKS = (256, 128, 128)
+
+FLOPS = 3 * 2 * 512 * 512 * 512
+
+
+def interleave(copy, grouped, planes):
+    copy(
+        out=grouped.rearrange("p (c i j) -> p c j i", i=4, j=PACK),
+        in_=planes.rearrange("p j (c i) -> p c j i", i=4),
+    )
+
+
+def tile_picked_momprod_none_po_kernel(
+    tc, x_words, x_scales, wa, wb, gt, gi, offs, two, fa, fb, out_0, out_1, out_2
+):
+    nc = tc.nc
+    with ExitStack() as ctx:
+        keep = ctx.enter_context(tc.tile_pool(name="keep", bufs=1))
+        psum = ctx.enter_context(tc.psum_pool(name="psum", bufs=1))
+
+        def sbuf(name, shape, dtype):
+            return keep.tile(shape, dtype, name=name, align_bytes=64)
+
+        def bank(index):
+            return psum.tile([P, BANK], F32, name="bank%d" % index)
+
+        def load_list(name, source):
+            tile = keep.tile([P, S // PER_COLUMN], U16, name=name)
+            nc.sync.dma_start(tile[:], source)
+            return tile
+
+        def load_weight_half(name, w, half):
+            tile = sbuf(name, [P, PACK, HALF], F32)
+            rows = w.rearrange("(p j) c -> p j c", j=PACK)
+            nc.sync.dma_start(tile[:], rows[:, :, half * HALF : (half + 1) * HALF])
+            return tile
+
+        def quantize(codes, scales, grouped):
+            nc.vector.quantize_mx(out=codes.bitcast(FP8X4), scales=scales, in_=grouped)
+
+        def product(out, lhs, lhs_cols, rhs, rhs_cols):
+            nc.tensor.matmul_mx(
+                out=out,
+                lhsT=lhs[0][:, lhs_cols].bitcast(FP8X4),
+                lhsT_scale=lhs[1][:, lhs_cols],
+                rhs=rhs[0][:, rhs_cols].bitcast(FP8X4),
+                rhs_scale=rhs[1][:, rhs_cols],
+                start=True,
+                stop=True,
+            )
+
+        table_scales = sbuf("table_scales", [P, T], U8)
+        nc.vector.memset(table_scales[:].bitcast(I32), 0)
+        offs_list = load_list("offs_list", offs)
+        two_list = load_list("two_list", two)
+        fa_list = load_list("fa_list", fa)
+        for q in range(4):
+            queue = nc.sync if q < 2 else nc.scalar
+            queue.dma_start(
+                table_scales[32 * q : 32 * q + 4, :].bitcast(I32),
+                x_scales[0, 4 * q : 4 * q + 4, :].bitcast(I32),
+            )
+        table_words = sbuf("table_words", [P, T], I32)
+        nc.sync.dma_start(table_words[:], x_words[0].rearrange("p c r -> p (c r)").bitcast(I32))
+        wa_raw = [load_weight_half("wa_raw%d" % h, wa, h) for h in range(2)]
+
+        identity = sbuf("identity", [P, P], F32)
+        make_identity(nc, identity[:])
+        warm = sbuf("warm", [P, 1], F32)
+        nc.scalar.activation(warm[:], identity[:, 0:1], ACT.Sigmoid)
+
+        weight_rows = sbuf("weight_rows", [P, P], F32)
+        nc.gpsimd.memset(weight_rows[:], 0.0)
+        for side, g in enumerate((gt, gi)):
+            nc.sync.dma_start(
+                weight_rows[PACK * side : PACK * (side + 1), :].rearrange("t (q r) -> t q r", r=8),
+                g.rearrange("(q t r) o -> t q (r o)", t=PACK, r=8),
+            )
+        wb_raw = [load_weight_half("wb_raw%d" % h, wb, h) for h in range(2)]
+        fb_list = load_list("fb_list", fb)
+
+        def pick_scales(name, token_list):
+            gathered = sbuf(name + "_listed", [P, S], U8)
+            nc.vector.tensor_copy(gathered[:], table_scales[:].indirect(token_list[:]))
+            return gathered
+
+        def deal_scales(name, gathered):
+            dealt = sbuf(name, [P, S], U8)
+            nc.vector.tensor_copy(
+                dealt[:].bitcast(I32).rearrange("p (t q w) -> p t q w", t=PACK, w=2),
+                gathered[:].bitcast(I32).rearrange("p (q t w) -> p t q w", t=PACK, w=2),
+            )
+            return dealt
+
+        def pick_words(name, token_list):
+            dealt = sbuf(name, [P, S], U32)
+            nc.vector.tensor_copy(
+                dealt[:].rearrange("p (t q r) -> p q t r", t=PACK, r=8),
+                table_words[:].bitcast(U32).indirect(token_list[:]),
+            )
+            return dealt
+
+        xa_listed = pick_scales("xa_scales", offs_list)
+        xb_listed = pick_scales("xb_scales", two_list)
+        xa_scales = deal_scales("xa_scales", xa_listed)
+        xb_scales = deal_scales("xb_scales", xb_listed)
+        xa = (pick_words("xa_words", offs_list), xa_scales)
+        xb = (pick_words("xb_words", two_list), xb_scales)
+
+        wa_q = (sbuf("wa_codes", [P, WIDTH], U32), sbuf("wa_scales", [P, WIDTH], U8))
+        wa_grouped = [sbuf("wa_grouped%d" % h, [P, PACK * HALF], BF16) for h in range(2)]
+        interleave(nc.scalar.copy, wa_grouped[0][:], wa_raw[0][:])
+        interleave(nc.scalar.copy, wa_grouped[1][:, : PACK * QUARTER], wa_raw[1][:, :, :QUARTER])
+        interleave(nc.vector.tensor_copy, wa_grouped[1][:, PACK * QUARTER :], wa_raw[1][:, :, QUARTER:])
+        a_banks = [bank(t) for t in range(PACK)]
+        for h in range(2):
+            cols = slice(h * HALF, (h + 1) * HALF)
+            quantize(wa_q[0][:, cols], wa_q[1][:, cols], wa_grouped[h][:])
+        for t in range(PACK):
+            for h in range(2):
+                cols = slice(h * HALF, (h + 1) * HALF)
+                product(a_banks[t][:, cols], xa, slice(t * P, (t + 1) * P), wa_q, cols)
+
+        wb_grouped = sbuf("wb_grouped", [P, PACK * WIDTH], BF16)
+        interleave(nc.scalar.copy, wb_grouped[:, : PACK * HALF], wb_raw[0][:])
+
+        turned = bank(7)
+        nc.tensor.transpose(turned[:, :P], weight_rows[:], identity[:])
+        place_weights = sbuf("place_weights", [P, 2 * PACK], F32)
+        nc.scalar.copy(place_weights[:], turned[:, : 2 * PACK])
+
+        a_rows = [sbuf("a_rows%d" % t, [P, WIDTH], F32) for t in range(PACK)]
+        a_gates = [sbuf("a_gates%d" % t, [P, WIDTH], F32) for t in range(PACK)]
+
+        def gate(out, rows, feature_list, start, stop):
+            offsets = feature_list[:, start // PER_COLUMN : stop // PER_COLUMN]
+            nc.scalar.activation(out, rows[:].indirect(offsets), ACT.Sigmoid)
+
+        for t in range(PACK):
+            nc.vector.tensor_copy(a_rows[t][:], a_banks[t][:])
+            for h in range(2):
+                gate(a_gates[t][:, h * HALF : (h + 1) * HALF], a_rows[t], fa_list, h * HALF, (h + 1) * HALF)
+
+        interleave(nc.vector.tensor_copy, wb_grouped[:, PACK * HALF :], wb_raw[1][:])
+        wb_q = (sbuf("wb_codes", [P, WIDTH], U32), sbuf("wb_scales", [P, WIDTH], U8))
+        quantize(wb_q[0][:], wb_q[1][:], wb_grouped[:])
+        b_banks = [bank(PACK + t) for t in range(PACK)]
+        b_rows = [sbuf("b_rows%d" % t, [P, WIDTH], F32) for t in range(PACK)]
+        for t in range(PACK):
+            product(b_banks[t][:], xb, slice(t * P, (t + 1) * P), wb_q, slice(0, WIDTH))
+            nc.scalar.copy(b_rows[t][:], b_banks[t][:])
+
+        def weigh(out, sums, column, gates):
+            nc.vector.scalar_tensor_tensor(out, sums, place_weights[:, column : column + 1], gates, MULT, MULT)
+
+        z_planes = sbuf("z_planes", [P, PACK, WIDTH], BF16)
+        for t in range(PACK):
+            weigh(z_planes[:, t, :], a_banks[t][:], t, a_gates[t][:])
+        z_grouped = sbuf("z_grouped", [P, PACK * WIDTH], BF16)
+        nc.vector.tensor_copy(
+            z_grouped[:].rearrange("p (u m i t) -> p m u i t", u=PACK, i=2, t=PACK),
+            z_planes[:].rearrange("p t (m i u) -> p m u i t", u=PACK, i=2),
+        )
+        z_q = (sbuf("z_codes", [P, WIDTH], U32), sbuf("z_scales", [P, WIDTH], U8))
+        quantize(z_q[0][:], z_q[1][:], z_grouped[:])
+
+        starts = [sum(CHUNKS[:c]) for c in range(len(CHUNKS))]
+        out_rows = out_0.rearrange("(p u) c -> p u c", u=PACK)
+        out_words = out_1[0].rearrange("p c r -> p (c r)").bitcast(I32)
+        y_scales = sbuf("y_scales", [P, WIDTH], U8)
+        results = []
+        next_bank = 0
+        for c, width in enumerate(CHUNKS):
+            cols = slice(starts[c], starts[c] + width)
+            z2_planes = sbuf("z2_planes%d" % c, [P, PACK, width], BF16)
+            for t in range(PACK):
+                gates = sbuf("b_gates%d_%d" % (c, t), [P, width], F32)
+                gate(gates[:], b_rows[t], fb_list, cols.start, cols.stop)
+                weigh(z2_planes[:, t, :], b_banks[t][:, cols], PACK + t, gates[:])
+            z2_grouped = sbuf("z2_grouped%d" % c, [P, PACK * width], BF16)
+            interleave(nc.vector.tensor_copy, z2_grouped[:], z2_planes[:])
+            z2_q = (sbuf("z2_codes%d" % c, [P, width], U32), sbuf("z2_scales%d" % c, [P, width], U8))
+            quantize(z2_q[0][:], z2_q[1][:], z2_grouped[:])
+            y = sbuf("y%d" % c, [P, PACK * width], F32)
+            per_bank = BANK // width
+            for first in range(0, PACK, per_bank):
+                sums = bank(next_bank)
+                next_bank = next_bank + 1
+                for k in range(per_bank):
+                    u = first + k
+                    product(sums[:, k * width : (k + 1) * width], z_q, slice(u * P, (u + 1) * P), z2_q, slice(0, width))
+                nc.scalar.activation(y[:, first * width : first * width + BANK], sums[:], ACT.Tanh, scale=0.0625)
+            nc.sync.dma_start(out_rows[:, :, cols], y[:].rearrange("p (u c) -> p u c", u=PACK))
+            results.append((cols, y))
+
+        for c, (cols, y) in enumerate(results):
+            width = CHUNKS[c]
+            y_grouped = sbuf("y_grouped%d" % c, [P, PACK * width], BF16)
+            interleave(nc.vector.tensor_copy, y_grouped[:], y[:].rearrange("p (u c) -> p u c", u=PACK))
+            y_codes = sbuf("y_codes%d" % c, [P, width], U32)
+            quantize(y_codes[:], y_scales[:, cols], y_grouped[:])
+            nc.sync.dma_start(out_words[:, cols], y_codes[:].bitcast(I32))
+        for q in range(4):
+            queue = nc.sync if q < 2 else nc.scalar
+            queue.dma_start(
+                out_2[0, 4 * q : 4 * q + 4, :].bitcast(I32),
+                y_scales[32 * q : 32 * q + 4, :].bitcast(I32),
+            )

@@ -12,6 +12,7 @@ U8 = mybir.dt.uint8
 FP8X4 = mybir.dt.float8_e4m3fn_x4
 ACT = mybir.ActivationFunctionType
 MULT = mybir.AluOpType.mult
+ADD = mybir.AluOpType.add
 
 P = 128
 PACK = 4
@@ -23,6 +24,7 @@ QUARTER = WIDTH // 4
 PER_COLUMN = 16
 BANK = 512
 CHUNKS = (256, 128, 128)
+GATHERS = {0: 256, 256: 128, 384: 128}
 
 FLOPS = 3 * 2 * 512 * 512 * 512
 
@@ -79,8 +81,7 @@ def tile_picked_momprod_none_po_kernel(
         two_list = load_list("two_list", two)
         fa_list = load_list("fa_list", fa)
         for q in range(4):
-            queue = nc.sync if q < 2 else nc.scalar
-            queue.dma_start(
+            nc.sync.dma_start(
                 table_scales[32 * q : 32 * q + 4, :].bitcast(I32),
                 x_scales[0, 4 * q : 4 * q + 4, :].bitcast(I32),
             )
@@ -102,6 +103,11 @@ def tile_picked_momprod_none_po_kernel(
             )
         wb_raw = [load_weight_half("wb_raw%d" % h, wb, h) for h in range(2)]
         fb_list = load_list("fb_list", fb)
+
+        a_rows = [sbuf("a_rows%d" % t, [P, 2 * WIDTH], F32) for t in range(PACK)]
+        b_rows = [sbuf("b_rows%d" % t, [P, WIDTH], F32) for t in range(PACK)]
+        for rows in a_rows:
+            nc.vector.memset(rows[:, WIDTH:], 0.0)
 
         def pick_scales(name, token_list):
             gathered = sbuf(name + "_listed", [P, S], U8)
@@ -141,50 +147,65 @@ def tile_picked_momprod_none_po_kernel(
             cols = slice(h * HALF, (h + 1) * HALF)
             quantize(wa_q[0][:, cols], wa_q[1][:, cols], wa_grouped[h][:])
         for t in range(PACK):
-            for h in range(2):
-                cols = slice(h * HALF, (h + 1) * HALF)
-                product(a_banks[t][:, cols], xa, slice(t * P, (t + 1) * P), wa_q, cols)
+            product(a_banks[t][:], xa, slice(t * P, (t + 1) * P), wa_q, slice(0, WIDTH))
 
         wb_grouped = sbuf("wb_grouped", [P, PACK * WIDTH], BF16)
         interleave(nc.scalar.copy, wb_grouped[:, : PACK * HALF], wb_raw[0][:])
+        nc.gpsimd.tensor_scalar(
+            wb_grouped[:, PACK * HALF :].rearrange("p (c j) -> p c j", j=PACK),
+            wb_raw[1][:].rearrange("p j c -> p c j"),
+            1.0,
+            0.0,
+            MULT,
+            ADD,
+        )
 
         turned = bank(7)
         nc.tensor.transpose(turned[:, :P], weight_rows[:], identity[:])
         place_weights = sbuf("place_weights", [P, 2 * PACK], F32)
         nc.scalar.copy(place_weights[:], turned[:, : 2 * PACK])
 
-        a_rows = [sbuf("a_rows%d" % t, [P, WIDTH], F32) for t in range(PACK)]
         a_gates = [sbuf("a_gates%d" % t, [P, WIDTH], F32) for t in range(PACK)]
 
         def gate(out, rows, feature_list, start, stop):
             offsets = feature_list[:, start // PER_COLUMN : stop // PER_COLUMN]
             nc.scalar.activation(out, rows[:].indirect(offsets), ACT.Sigmoid)
 
-        for t in range(PACK):
-            nc.vector.tensor_copy(a_rows[t][:], a_banks[t][:])
-            for h in range(2):
-                gate(a_gates[t][:, h * HALF : (h + 1) * HALF], a_rows[t], fa_list, h * HALF, (h + 1) * HALF)
-
-        interleave(nc.vector.tensor_copy, wb_grouped[:, PACK * HALF :], wb_raw[1][:])
-        wb_q = (sbuf("wb_codes", [P, WIDTH], U32), sbuf("wb_scales", [P, WIDTH], U8))
-        quantize(wb_q[0][:], wb_q[1][:], wb_grouped[:])
-        b_banks = [bank(PACK + t) for t in range(PACK)]
-        b_rows = [sbuf("b_rows%d" % t, [P, WIDTH], F32) for t in range(PACK)]
-        for t in range(PACK):
-            product(b_banks[t][:], xb, slice(t * P, (t + 1) * P), wb_q, slice(0, WIDTH))
-            nc.scalar.copy(b_rows[t][:], b_banks[t][:])
-
         def weigh(out, sums, column, gates):
             nc.vector.scalar_tensor_tensor(out, sums, place_weights[:, column : column + 1], gates, MULT, MULT)
 
+        def a_window(t):
+            nc.vector.tensor_copy(a_rows[t][:, :WIDTH], a_banks[t][:])
+            gate(a_gates[t][:], a_rows[t], fa_list, 0, WIDTH)
+
+        wb_q = (sbuf("wb_codes", [P, WIDTH], U32), sbuf("wb_scales", [P, WIDTH], U8))
+        b_banks = [bank(PACK + t) for t in range(PACK)]
         z_planes = sbuf("z_planes", [P, PACK, WIDTH], BF16)
+
+        a_window(0)
+        a_window(1)
+        quantize(wb_q[0][:], wb_q[1][:], wb_grouped[:])
         for t in range(PACK):
-            weigh(z_planes[:, t, :], a_banks[t][:], t, a_gates[t][:])
+            product(b_banks[t][:], xb, slice(t * P, (t + 1) * P), wb_q, slice(0, WIDTH))
+        a_window(2)
+        a_window(3)
+        weigh(z_planes[:, 0, :], a_banks[0][:], 0, a_gates[0][:])
+        for t in range(PACK):
+            if t + 1 < PACK:
+                weigh(z_planes[:, t + 1, :], a_banks[t + 1][:], t + 1, a_gates[t + 1][:])
+            nc.vector.tensor_copy(b_rows[t][:, :WIDTH], b_banks[t][:])
+
         z_grouped = sbuf("z_grouped", [P, PACK * WIDTH], BF16)
-        nc.vector.tensor_copy(
-            z_grouped[:].rearrange("p (u m i t) -> p m u i t", u=PACK, i=2, t=PACK),
-            z_planes[:].rearrange("p t (m i u) -> p m u i t", u=PACK, i=2),
-        )
+        z_dealt = z_planes[:].rearrange("p t (m u) -> p u m t", u=PACK)
+        for h in range(2):
+            nc.gpsimd.tensor_scalar(
+                z_grouped[:, h * PACK * HALF : (h + 1) * PACK * HALF].rearrange("p (u m t) -> p u m t", u=2, t=PACK),
+                z_dealt[:, 2 * h : 2 * h + 2, :, :],
+                1.0,
+                0.0,
+                MULT,
+                ADD,
+            )
         z_q = (sbuf("z_codes", [P, WIDTH], U32), sbuf("z_scales", [P, WIDTH], U8))
         quantize(z_q[0][:], z_q[1][:], z_grouped[:])
 
@@ -196,13 +217,16 @@ def tile_picked_momprod_none_po_kernel(
         next_bank = 0
         for c, width in enumerate(CHUNKS):
             cols = slice(starts[c], starts[c] + width)
-            z2_planes = sbuf("z2_planes%d" % c, [P, PACK, width], BF16)
-            for t in range(PACK):
-                gates = sbuf("b_gates%d_%d" % (c, t), [P, width], F32)
-                gate(gates[:], b_rows[t], fb_list, cols.start, cols.stop)
-                weigh(z2_planes[:, t, :], b_banks[t][:, cols], PACK + t, gates[:])
+            if cols.start in GATHERS:
+                span = GATHERS[cols.start]
+                base = cols.start
+                z2_planes = sbuf("z2_planes%d" % c, [P, PACK, span], BF16)
+                for t in range(PACK):
+                    gates = sbuf("b_gates%d_%d" % (c, t), [P, span], F32)
+                    gate(gates[:], b_rows[t], fb_list, base, base + span)
+                    weigh(z2_planes[:, t, :], b_banks[t][:, base : base + span], PACK + t, gates[:])
             z2_grouped = sbuf("z2_grouped%d" % c, [P, PACK * width], BF16)
-            interleave(nc.vector.tensor_copy, z2_grouped[:], z2_planes[:])
+            interleave(nc.vector.tensor_copy, z2_grouped[:], z2_planes[:, :, cols.start - base : cols.stop - base])
             z2_q = (sbuf("z2_codes%d" % c, [P, width], U32), sbuf("z2_scales%d" % c, [P, width], U8))
             quantize(z2_q[0][:], z2_q[1][:], z2_grouped[:])
             y = sbuf("y%d" % c, [P, PACK * width], F32)
@@ -225,8 +249,7 @@ def tile_picked_momprod_none_po_kernel(
             quantize(y_codes[:], y_scales[:, cols], y_grouped[:])
             nc.sync.dma_start(out_words[:, cols], y_codes[:].bitcast(I32))
         for q in range(4):
-            queue = nc.sync if q < 2 else nc.scalar
-            queue.dma_start(
+            nc.sync.dma_start(
                 out_2[0, 4 * q : 4 * q + 4, :].bitcast(I32),
                 y_scales[32 * q : 32 * q + 4, :].bitcast(I32),
             )

@@ -24,7 +24,6 @@ QUARTER = WIDTH // 4
 PER_COLUMN = 16
 BANK = 512
 CHUNKS = (256, 128, 128)
-GATHERS = {0: 256, 256: 128, 384: 128}
 
 FLOPS = 3 * 2 * 512 * 512 * 512
 
@@ -42,6 +41,8 @@ def tile_picked_momprod_none_po_kernel(
     nc = tc.nc
     with ExitStack() as ctx:
         keep = ctx.enter_context(tc.tile_pool(name="keep", bufs=1))
+        reused = ctx.enter_context(tc.tile_pool(name="reused", bufs=1))
+        ring = ctx.enter_context(tc.tile_pool(name="ring", bufs=5))
         psum = ctx.enter_context(tc.psum_pool(name="psum", bufs=1))
 
         def sbuf(name, shape, dtype):
@@ -109,45 +110,40 @@ def tile_picked_momprod_none_po_kernel(
         for rows in a_rows:
             nc.vector.memset(rows[:, WIDTH:], 0.0)
 
-        def pick_scales(name, token_list):
-            gathered = sbuf(name + "_listed", [P, S], U8)
-            nc.vector.tensor_copy(gathered[:], table_scales[:].indirect(token_list[:]))
-            return gathered
-
-        def deal_scales(name, gathered):
+        def pick_scales(name, listed, token_list):
+            nc.vector.tensor_copy(listed[:], table_scales[:].indirect(token_list[:]))
             dealt = sbuf(name, [P, S], U8)
             nc.vector.tensor_copy(
                 dealt[:].bitcast(I32).rearrange("p (t q w) -> p t q w", t=PACK, w=2),
-                gathered[:].bitcast(I32).rearrange("p (q t w) -> p t q w", t=PACK, w=2),
+                listed[:].bitcast(I32).rearrange("p (q t w) -> p t q w", t=PACK, w=2),
             )
             return dealt
 
-        def pick_words(name, token_list):
-            dealt = sbuf(name, [P, S], U32)
+        def pick_words(dealt, token_list):
             nc.vector.tensor_copy(
                 dealt[:].rearrange("p (t q r) -> p q t r", t=PACK, r=8),
                 table_words[:].bitcast(U32).indirect(token_list[:]),
             )
             return dealt
 
-        xa_listed = pick_scales("xa_scales", offs_list)
-        xb_listed = pick_scales("xb_scales", two_list)
-        xa_scales = deal_scales("xa_scales", xa_listed)
-        xb_scales = deal_scales("xb_scales", xb_listed)
-        xa = (pick_words("xa_words", offs_list), xa_scales)
-        xb = (pick_words("xb_words", two_list), xb_scales)
+        xa_scales = pick_scales("xa_scales", sbuf("xa_listed", [P, S], U8), offs_list)
+        xb_scales = pick_scales("xb_scales", sbuf("xb_listed", [P, S], U8), two_list)
+        xa = (pick_words(sbuf("xa_words", [P, S], U32), offs_list), xa_scales)
 
         wa_q = (sbuf("wa_codes", [P, WIDTH], U32), sbuf("wa_scales", [P, WIDTH], U8))
-        wa_grouped = [sbuf("wa_grouped%d" % h, [P, PACK * HALF], BF16) for h in range(2)]
-        interleave(nc.scalar.copy, wa_grouped[0][:], wa_raw[0][:])
-        interleave(nc.scalar.copy, wa_grouped[1][:, : PACK * QUARTER], wa_raw[1][:, :, :QUARTER])
-        interleave(nc.vector.tensor_copy, wa_grouped[1][:, PACK * QUARTER :], wa_raw[1][:, :, QUARTER:])
+        wa_grouped = reused.tile([P, PACK * WIDTH], BF16, name="wa_grouped", align_bytes=64, offset=0)
+        split = PACK * (HALF + QUARTER)
+        interleave(nc.scalar.copy, wa_grouped[:, : PACK * HALF], wa_raw[0][:])
+        interleave(nc.scalar.copy, wa_grouped[:, PACK * HALF : split], wa_raw[1][:, :, :QUARTER])
+        interleave(nc.vector.tensor_copy, wa_grouped[:, split:], wa_raw[1][:, :, QUARTER:])
         a_banks = [bank(t) for t in range(PACK)]
         for h in range(2):
             cols = slice(h * HALF, (h + 1) * HALF)
-            quantize(wa_q[0][:, cols], wa_q[1][:, cols], wa_grouped[h][:])
+            quantize(wa_q[0][:, cols], wa_q[1][:, cols], wa_grouped[:, PACK * cols.start : PACK * cols.stop])
         for t in range(PACK):
             product(a_banks[t][:], xa, slice(t * P, (t + 1) * P), wa_q, slice(0, WIDTH))
+
+        xb = (pick_words(reused.tile([P, S], U32, name="xb_words", align_bytes=64, offset=0), two_list), xb_scales)
 
         wb_grouped = sbuf("wb_grouped", [P, PACK * WIDTH], BF16)
         interleave(nc.scalar.copy, wb_grouped[:, : PACK * HALF], wb_raw[0][:])
@@ -175,25 +171,25 @@ def tile_picked_momprod_none_po_kernel(
             nc.vector.scalar_tensor_tensor(out, sums, place_weights[:, column : column + 1], gates, MULT, MULT)
 
         def a_window(t):
-            nc.vector.tensor_copy(a_rows[t][:, :WIDTH], a_banks[t][:])
+            copy = nc.scalar.copy if t == 0 else nc.vector.tensor_copy
+            copy(a_rows[t][:, :WIDTH], a_banks[t][:])
             gate(a_gates[t][:], a_rows[t], fa_list, 0, WIDTH)
 
         wb_q = (sbuf("wb_codes", [P, WIDTH], U32), sbuf("wb_scales", [P, WIDTH], U8))
         b_banks = [bank(PACK + t) for t in range(PACK)]
         z_planes = sbuf("z_planes", [P, PACK, WIDTH], BF16)
 
-        a_window(0)
-        a_window(1)
+        for t in range(PACK - 1):
+            a_window(t)
         quantize(wb_q[0][:], wb_q[1][:], wb_grouped[:])
         for t in range(PACK):
             product(b_banks[t][:], xb, slice(t * P, (t + 1) * P), wb_q, slice(0, WIDTH))
-        a_window(2)
-        a_window(3)
+        a_window(PACK - 1)
         weigh(z_planes[:, 0, :], a_banks[0][:], 0, a_gates[0][:])
-        for t in range(PACK):
-            if t + 1 < PACK:
-                weigh(z_planes[:, t + 1, :], a_banks[t + 1][:], t + 1, a_gates[t + 1][:])
-            nc.vector.tensor_copy(b_rows[t][:, :WIDTH], b_banks[t][:])
+        for t in range(1, PACK):
+            weigh(z_planes[:, t, :], a_banks[t][:], t, a_gates[t][:])
+            nc.vector.tensor_copy(b_rows[t - 1][:], b_banks[t - 1][:])
+        nc.vector.tensor_copy(b_rows[PACK - 1][:], b_banks[PACK - 1][:])
 
         z_grouped = sbuf("z_grouped", [P, PACK * WIDTH], BF16)
         z_dealt = z_planes[:].rearrange("p t (m u) -> p u m t", u=PACK)
@@ -213,43 +209,57 @@ def tile_picked_momprod_none_po_kernel(
         out_rows = out_0.rearrange("(p u) c -> p u c", u=PACK)
         out_words = out_1[0].rearrange("p c r -> p (c r)").bitcast(I32)
         y_scales = sbuf("y_scales", [P, WIDTH], U8)
-        results = []
-        next_bank = 0
+        pending = []
         for c, width in enumerate(CHUNKS):
             cols = slice(starts[c], starts[c] + width)
-            if cols.start in GATHERS:
-                span = GATHERS[cols.start]
-                base = cols.start
-                z2_planes = sbuf("z2_planes%d" % c, [P, PACK, span], BF16)
-                for t in range(PACK):
-                    gates = sbuf("b_gates%d_%d" % (c, t), [P, span], F32)
-                    gate(gates[:], b_rows[t], fb_list, base, base + span)
-                    weigh(z2_planes[:, t, :], b_banks[t][:, base : base + span], PACK + t, gates[:])
+            z2_planes = sbuf("z2_planes%d" % c, [P, PACK, width], BF16)
+            for t in range(PACK):
+                gates = ring.tile([P, width], F32, name="b_gates")
+                gate(gates[:], b_rows[t], fb_list, cols.start, cols.stop)
+                weigh(z2_planes[:, t, :], b_banks[t][:, cols], PACK + t, gates[:])
             z2_grouped = sbuf("z2_grouped%d" % c, [P, PACK * width], BF16)
-            interleave(nc.vector.tensor_copy, z2_grouped[:], z2_planes[:, :, cols.start - base : cols.stop - base])
+            interleave(nc.vector.tensor_copy, z2_grouped[:], z2_planes[:])
             z2_q = (sbuf("z2_codes%d" % c, [P, width], U32), sbuf("z2_scales%d" % c, [P, width], U8))
             quantize(z2_q[0][:], z2_q[1][:], z2_grouped[:])
-            y = sbuf("y%d" % c, [P, PACK * width], F32)
             per_bank = BANK // width
             for first in range(0, PACK, per_bank):
-                sums = bank(next_bank)
-                next_bank = next_bank + 1
+                sums = bank(len(pending))
                 for k in range(per_bank):
                     u = first + k
                     product(sums[:, k * width : (k + 1) * width], z_q, slice(u * P, (u + 1) * P), z2_q, slice(0, width))
-                nc.scalar.activation(y[:, first * width : first * width + BANK], sums[:], ACT.Tanh, scale=0.0625)
-            nc.sync.dma_start(out_rows[:, :, cols], y[:].rearrange("p (u c) -> p u c", u=PACK))
-            results.append((cols, y))
+                pending.append((c, cols, first, sums))
 
-        for c, (cols, y) in enumerate(results):
+        ys = [sbuf("y%d" % c, [P, PACK * width], F32) for c, width in enumerate(CHUNKS)]
+        for c, cols, first, sums in pending:
             width = CHUNKS[c]
-            y_grouped = sbuf("y_grouped%d" % c, [P, PACK * width], BF16)
-            interleave(nc.vector.tensor_copy, y_grouped[:], y[:].rearrange("p (u c) -> p u c", u=PACK))
-            y_codes = sbuf("y_codes%d" % c, [P, width], U32)
-            quantize(y_codes[:], y_scales[:, cols], y_grouped[:])
-            nc.sync.dma_start(out_words[:, cols], y_codes[:].bitcast(I32))
-        for q in range(4):
+            if c == len(CHUNKS) - 1:
+                last_grouped = sbuf("y_grouped%d" % c, [P, PACK * width], BF16)
+                nc.scalar.activation(
+                    last_grouped[:].rearrange("p (c u) -> p c u", u=PACK),
+                    sums[:].rearrange("p (u c) -> p c u", u=PACK),
+                    ACT.Tanh,
+                    scale=0.0625,
+                )
+            part = ys[c][:, first * width : first * width + BANK]
+            nc.scalar.activation(part, sums[:], ACT.Tanh, scale=0.0625)
             nc.sync.dma_start(
+                out_rows[:, first : first + BANK // width, cols], part.rearrange("p (u c) -> p u c", c=width)
+            )
+        results = [(slice(starts[c], starts[c] + width), ys[c]) for c, width in enumerate(CHUNKS)]
+
+        y_codes = sbuf("y_codes", [P, WIDTH], U32)
+        for c, (cols, y) in enumerate(results[:-1]):
+            y_grouped = sbuf("y_grouped%d" % c, [P, PACK * CHUNKS[c]], BF16)
+            interleave(nc.vector.tensor_copy, y_grouped[:], y[:].rearrange("p (u c) -> p u c", u=PACK))
+            quantize(y_codes[:, cols], y_scales[:, cols], y_grouped[:])
+        early = slice(0, starts[-1])
+        late = slice(starts[-1], WIDTH)
+        nc.sync.dma_start(out_words[:, early], y_codes[:, early].bitcast(I32))
+        quantize(y_codes[:, late], y_scales[:, late], last_grouped[:])
+        nc.scalar.dma_start(out_words[:, late], y_codes[:, late].bitcast(I32))
+        for q in range(4):
+            queue = nc.sync if q < 3 else nc.scalar
+            queue.dma_start(
                 out_2[0, 4 * q : 4 * q + 4, :].bitcast(I32),
                 y_scales[32 * q : 32 * q + 4, :].bitcast(I32),
             )

@@ -1,7 +1,6 @@
 from contextlib import ExitStack
 
 import concourse.mybir as mybir
-from concourse.masks import make_identity
 
 F32 = mybir.dt.float32
 BF16 = mybir.dt.bfloat16
@@ -16,6 +15,7 @@ ADD = mybir.AluOpType.add
 
 P = 128
 PACK = 4
+QUADRANTS = 4
 T = 2048
 S = 512
 WIDTH = 512
@@ -24,6 +24,8 @@ QUARTER = WIDTH // 4
 PER_COLUMN = 16
 BANK = 512
 CHUNKS = (256, 128, 128)
+GATE_TILES = 5
+CV_SCALE = 0.0625
 
 FLOPS = 3 * 2 * 512 * 512 * 512
 
@@ -42,7 +44,7 @@ def tile_picked_momprod_none_po_kernel(
     with ExitStack() as ctx:
         keep = ctx.enter_context(tc.tile_pool(name="keep", bufs=1))
         reused = ctx.enter_context(tc.tile_pool(name="reused", bufs=1))
-        ring = ctx.enter_context(tc.tile_pool(name="ring", bufs=5))
+        ring = ctx.enter_context(tc.tile_pool(name="ring", bufs=GATE_TILES))
         psum = ctx.enter_context(tc.psum_pool(name="psum", bufs=1))
 
         def sbuf(name, shape, dtype):
@@ -62,16 +64,22 @@ def tile_picked_momprod_none_po_kernel(
             nc.sync.dma_start(tile[:], rows[:, :, half * HALF : (half + 1) * HALF])
             return tile
 
+        def load_place_weights(name, g):
+            tile = sbuf(name, [P, PACK], F32)
+            nc.sync.dma_start(tile[:], g.rearrange("(p j) o -> p (j o)", j=PACK))
+            return tile
+
         def quantize(codes, scales, grouped):
             nc.vector.quantize_mx(out=codes.bitcast(FP8X4), scales=scales, in_=grouped)
 
-        def product(out, lhs, lhs_cols, rhs, rhs_cols):
+        def product(out, stationary, plane, moving):
+            cols = slice(plane * P, (plane + 1) * P)
             nc.tensor.matmul_mx(
                 out=out,
-                lhsT=lhs[0][:, lhs_cols].bitcast(FP8X4),
-                lhsT_scale=lhs[1][:, lhs_cols],
-                rhs=rhs[0][:, rhs_cols].bitcast(FP8X4),
-                rhs_scale=rhs[1][:, rhs_cols],
+                lhsT=stationary[0][:, cols].bitcast(FP8X4),
+                lhsT_scale=stationary[1][:, cols],
+                rhs=moving[0][:].bitcast(FP8X4),
+                rhs_scale=moving[1][:],
                 start=True,
                 stop=True,
             )
@@ -81,7 +89,7 @@ def tile_picked_momprod_none_po_kernel(
         offs_list = load_list("offs_list", offs)
         two_list = load_list("two_list", two)
         fa_list = load_list("fa_list", fa)
-        for q in range(4):
+        for q in range(QUADRANTS):
             nc.sync.dma_start(
                 table_scales[32 * q : 32 * q + 4, :].bitcast(I32),
                 x_scales[0, 4 * q : 4 * q + 4, :].bitcast(I32),
@@ -89,45 +97,38 @@ def tile_picked_momprod_none_po_kernel(
         table_words = sbuf("table_words", [P, T], I32)
         nc.sync.dma_start(table_words[:], x_words[0].rearrange("p c r -> p (c r)").bitcast(I32))
         wa_raw = [load_weight_half("wa_raw%d" % h, wa, h) for h in range(2)]
-
-        identity = sbuf("identity", [P, P], F32)
-        make_identity(nc, identity[:])
-        warm = sbuf("warm", [P, 1], F32)
-        nc.scalar.activation(warm[:], identity[:, 0:1], ACT.Sigmoid)
-
-        weight_rows = sbuf("weight_rows", [P, P], F32)
-        nc.gpsimd.memset(weight_rows[:], 0.0)
-        for side, g in enumerate((gt, gi)):
-            nc.sync.dma_start(
-                weight_rows[PACK * side : PACK * (side + 1), :].rearrange("t (q r) -> t q r", r=8),
-                g.rearrange("(q t r) o -> t q (r o)", t=PACK, r=8),
-            )
         wb_raw = [load_weight_half("wb_raw%d" % h, wb, h) for h in range(2)]
+        gt_places = load_place_weights("gt_places", gt)
+        gi_places = load_place_weights("gi_places", gi)
         fb_list = load_list("fb_list", fb)
 
-        a_rows = [sbuf("a_rows%d" % t, [P, 2 * WIDTH], F32) for t in range(PACK)]
-        b_rows = [sbuf("b_rows%d" % t, [P, WIDTH], F32) for t in range(PACK)]
+        a_rows = [sbuf("a_rows%d" % j, [P, 2 * WIDTH], F32) for j in range(PACK)]
+        b_rows = [sbuf("b_rows%d" % j, [P, WIDTH], F32) for j in range(PACK)]
         for rows in a_rows:
             nc.vector.memset(rows[:, WIDTH:], 0.0)
 
-        def pick_scales(name, listed, token_list):
+        warm = sbuf("warm", [P, 1], F32)
+        nc.scalar.activation(warm[:], a_rows[0][:, WIDTH : WIDTH + 1], ACT.Sigmoid)
+
+        def pick_scales(name, token_list):
+            listed = sbuf(name + "_listed", [P, S], U8)
             nc.vector.tensor_copy(listed[:], table_scales[:].indirect(token_list[:]))
             dealt = sbuf(name, [P, S], U8)
             nc.vector.tensor_copy(
-                dealt[:].bitcast(I32).rearrange("p (t q w) -> p t q w", t=PACK, w=2),
-                listed[:].bitcast(I32).rearrange("p (q t w) -> p t q w", t=PACK, w=2),
+                dealt[:].rearrange("p (j m) -> p j m", j=PACK),
+                listed[:].rearrange("p (m j) -> p j m", j=PACK),
             )
             return dealt
 
         def pick_words(dealt, token_list):
             nc.vector.tensor_copy(
-                dealt[:].rearrange("p (t q r) -> p q t r", t=PACK, r=8),
+                dealt[:].rearrange("p (j m) -> p m j", j=PACK),
                 table_words[:].bitcast(U32).indirect(token_list[:]),
             )
             return dealt
 
-        xa_scales = pick_scales("xa_scales", sbuf("xa_listed", [P, S], U8), offs_list)
-        xb_scales = pick_scales("xb_scales", sbuf("xb_listed", [P, S], U8), two_list)
+        xa_scales = pick_scales("xa_scales", offs_list)
+        xb_scales = pick_scales("xb_scales", two_list)
         xa = (pick_words(sbuf("xa_words", [P, S], U32), offs_list), xa_scales)
 
         wa_q = (sbuf("wa_codes", [P, WIDTH], U32), sbuf("wa_scales", [P, WIDTH], U8))
@@ -136,14 +137,15 @@ def tile_picked_momprod_none_po_kernel(
         interleave(nc.scalar.copy, wa_grouped[:, : PACK * HALF], wa_raw[0][:])
         interleave(nc.scalar.copy, wa_grouped[:, PACK * HALF : split], wa_raw[1][:, :, :QUARTER])
         interleave(nc.vector.tensor_copy, wa_grouped[:, split:], wa_raw[1][:, :, QUARTER:])
-        a_banks = [bank(t) for t in range(PACK)]
+        a_banks = [bank(j) for j in range(PACK)]
         for h in range(2):
             cols = slice(h * HALF, (h + 1) * HALF)
             quantize(wa_q[0][:, cols], wa_q[1][:, cols], wa_grouped[:, PACK * cols.start : PACK * cols.stop])
-        for t in range(PACK):
-            product(a_banks[t][:], xa, slice(t * P, (t + 1) * P), wa_q, slice(0, WIDTH))
+        for j in range(PACK):
+            product(a_banks[j][:], xa, j, wa_q)
 
-        xb = (pick_words(reused.tile([P, S], U32, name="xb_words", align_bytes=64, offset=0), two_list), xb_scales)
+        xb_words = reused.tile([P, S], U32, name="xb_words", align_bytes=64, offset=0)
+        xb = (pick_words(xb_words, two_list), xb_scales)
 
         wb_grouped = sbuf("wb_grouped", [P, PACK * WIDTH], BF16)
         interleave(nc.scalar.copy, wb_grouped[:, : PACK * HALF], wb_raw[0][:])
@@ -156,109 +158,97 @@ def tile_picked_momprod_none_po_kernel(
             ADD,
         )
 
-        turned = bank(7)
-        nc.tensor.transpose(turned[:, :P], weight_rows[:], identity[:])
-        place_weights = sbuf("place_weights", [P, 2 * PACK], F32)
-        nc.scalar.copy(place_weights[:], turned[:, : 2 * PACK])
-
-        a_gates = [sbuf("a_gates%d" % t, [P, WIDTH], F32) for t in range(PACK)]
-
-        def gate(out, rows, feature_list, start, stop):
-            offsets = feature_list[:, start // PER_COLUMN : stop // PER_COLUMN]
+        def gate(out, rows, feature_list, cols):
+            offsets = feature_list[:, cols.start // PER_COLUMN : cols.stop // PER_COLUMN]
             nc.scalar.activation(out, rows[:].indirect(offsets), ACT.Sigmoid)
 
-        def weigh(out, sums, column, gates):
-            nc.vector.scalar_tensor_tensor(out, sums, place_weights[:, column : column + 1], gates, MULT, MULT)
+        def weigh(out, sums, places, j, gates):
+            nc.vector.scalar_tensor_tensor(out, sums, places[:, j : j + 1], gates, MULT, MULT)
 
-        def a_window(t):
-            copy = nc.scalar.copy if t == 0 else nc.vector.tensor_copy
-            copy(a_rows[t][:, :WIDTH], a_banks[t][:])
-            gate(a_gates[t][:], a_rows[t], fa_list, 0, WIDTH)
+        a_gates = [sbuf("a_gates%d" % j, [P, WIDTH], F32) for j in range(PACK)]
+
+        def gate_a(j):
+            copy = nc.scalar.copy if j == 0 else nc.vector.tensor_copy
+            copy(a_rows[j][:, :WIDTH], a_banks[j][:])
+            gate(a_gates[j][:], a_rows[j], fa_list, slice(0, WIDTH))
 
         wb_q = (sbuf("wb_codes", [P, WIDTH], U32), sbuf("wb_scales", [P, WIDTH], U8))
-        b_banks = [bank(PACK + t) for t in range(PACK)]
+        b_banks = [bank(PACK + j) for j in range(PACK)]
         z_planes = sbuf("z_planes", [P, PACK, WIDTH], BF16)
 
-        for t in range(PACK - 1):
-            a_window(t)
+        for j in range(PACK - 1):
+            gate_a(j)
         quantize(wb_q[0][:], wb_q[1][:], wb_grouped[:])
-        for t in range(PACK):
-            product(b_banks[t][:], xb, slice(t * P, (t + 1) * P), wb_q, slice(0, WIDTH))
-        a_window(PACK - 1)
-        weigh(z_planes[:, 0, :], a_banks[0][:], 0, a_gates[0][:])
-        for t in range(1, PACK):
-            weigh(z_planes[:, t, :], a_banks[t][:], t, a_gates[t][:])
-            nc.vector.tensor_copy(b_rows[t - 1][:], b_banks[t - 1][:])
+        for j in range(PACK):
+            product(b_banks[j][:], xb, j, wb_q)
+        gate_a(PACK - 1)
+        weigh(z_planes[:, 0, :], a_banks[0][:], gt_places, 0, a_gates[0][:])
+        for j in range(1, PACK):
+            weigh(z_planes[:, j, :], a_banks[j][:], gt_places, j, a_gates[j][:])
+            nc.vector.tensor_copy(b_rows[j - 1][:], b_banks[j - 1][:])
         nc.vector.tensor_copy(b_rows[PACK - 1][:], b_banks[PACK - 1][:])
 
         z_grouped = sbuf("z_grouped", [P, PACK * WIDTH], BF16)
-        z_dealt = z_planes[:].rearrange("p t (m u) -> p u m t", u=PACK)
-        for h in range(2):
-            nc.gpsimd.tensor_scalar(
-                z_grouped[:, h * PACK * HALF : (h + 1) * PACK * HALF].rearrange("p (u m t) -> p u m t", u=2, t=PACK),
-                z_dealt[:, 2 * h : 2 * h + 2, :, :],
-                1.0,
-                0.0,
-                MULT,
-                ADD,
-            )
+        nc.vector.tensor_copy(
+            z_grouped[:].rearrange("p (u m i j) -> p m u i j", u=PACK, i=2, j=PACK),
+            z_planes[:].rearrange("p j (m i u) -> p m u i j", u=PACK, i=2),
+        )
         z_q = (sbuf("z_codes", [P, WIDTH], U32), sbuf("z_scales", [P, WIDTH], U8))
         quantize(z_q[0][:], z_q[1][:], z_grouped[:])
 
-        starts = [sum(CHUNKS[:c]) for c in range(len(CHUNKS))]
+        chunk_cols = [slice(sum(CHUNKS[:c]), sum(CHUNKS[: c + 1])) for c in range(len(CHUNKS))]
+        last = len(CHUNKS) - 1
         out_rows = out_0.rearrange("(p u) c -> p u c", u=PACK)
         out_words = out_1[0].rearrange("p c r -> p (c r)").bitcast(I32)
         y_scales = sbuf("y_scales", [P, WIDTH], U8)
-        pending = []
+        filled = []
         for c, width in enumerate(CHUNKS):
-            cols = slice(starts[c], starts[c] + width)
             z2_planes = sbuf("z2_planes%d" % c, [P, PACK, width], BF16)
-            for t in range(PACK):
+            for j in range(PACK):
                 gates = ring.tile([P, width], F32, name="b_gates")
-                gate(gates[:], b_rows[t], fb_list, cols.start, cols.stop)
-                weigh(z2_planes[:, t, :], b_banks[t][:, cols], PACK + t, gates[:])
+                gate(gates[:], b_rows[j], fb_list, chunk_cols[c])
+                weigh(z2_planes[:, j, :], b_banks[j][:, chunk_cols[c]], gi_places, j, gates[:])
             z2_grouped = sbuf("z2_grouped%d" % c, [P, PACK * width], BF16)
             interleave(nc.vector.tensor_copy, z2_grouped[:], z2_planes[:])
             z2_q = (sbuf("z2_codes%d" % c, [P, width], U32), sbuf("z2_scales%d" % c, [P, width], U8))
             quantize(z2_q[0][:], z2_q[1][:], z2_grouped[:])
             per_bank = BANK // width
             for first in range(0, PACK, per_bank):
-                sums = bank(len(pending))
+                sums = bank(len(filled))
                 for k in range(per_bank):
-                    u = first + k
-                    product(sums[:, k * width : (k + 1) * width], z_q, slice(u * P, (u + 1) * P), z2_q, slice(0, width))
-                pending.append((c, cols, first, sums))
+                    product(sums[:, k * width : (k + 1) * width], z_q, first + k, z2_q)
+                filled.append((c, first, sums))
 
         ys = [sbuf("y%d" % c, [P, PACK * width], F32) for c, width in enumerate(CHUNKS)]
-        for c, cols, first, sums in pending:
+        for c, first, sums in filled:
             width = CHUNKS[c]
-            if c == len(CHUNKS) - 1:
+            if c == last:
                 last_grouped = sbuf("y_grouped%d" % c, [P, PACK * width], BF16)
                 nc.scalar.activation(
                     last_grouped[:].rearrange("p (c u) -> p c u", u=PACK),
                     sums[:].rearrange("p (u c) -> p c u", u=PACK),
                     ACT.Tanh,
-                    scale=0.0625,
+                    scale=CV_SCALE,
                 )
             part = ys[c][:, first * width : first * width + BANK]
-            nc.scalar.activation(part, sums[:], ACT.Tanh, scale=0.0625)
+            nc.scalar.activation(part, sums[:], ACT.Tanh, scale=CV_SCALE)
             nc.sync.dma_start(
-                out_rows[:, first : first + BANK // width, cols], part.rearrange("p (u c) -> p u c", c=width)
+                out_rows[:, first : first + BANK // width, chunk_cols[c]],
+                part.rearrange("p (u c) -> p u c", c=width),
             )
-        results = [(slice(starts[c], starts[c] + width), ys[c]) for c, width in enumerate(CHUNKS)]
 
         y_codes = sbuf("y_codes", [P, WIDTH], U32)
-        for c, (cols, y) in enumerate(results[:-1]):
+        for c in range(last):
             y_grouped = sbuf("y_grouped%d" % c, [P, PACK * CHUNKS[c]], BF16)
-            interleave(nc.vector.tensor_copy, y_grouped[:], y[:].rearrange("p (u c) -> p u c", u=PACK))
-            quantize(y_codes[:, cols], y_scales[:, cols], y_grouped[:])
-        early = slice(0, starts[-1])
-        late = slice(starts[-1], WIDTH)
+            interleave(nc.vector.tensor_copy, y_grouped[:], ys[c][:].rearrange("p (u c) -> p u c", u=PACK))
+            quantize(y_codes[:, chunk_cols[c]], y_scales[:, chunk_cols[c]], y_grouped[:])
+        early = slice(0, chunk_cols[last].start)
+        late = chunk_cols[last]
         nc.sync.dma_start(out_words[:, early], y_codes[:, early].bitcast(I32))
         quantize(y_codes[:, late], y_scales[:, late], last_grouped[:])
         nc.scalar.dma_start(out_words[:, late], y_codes[:, late].bitcast(I32))
-        for q in range(4):
-            queue = nc.sync if q < 3 else nc.scalar
+        for q in range(QUADRANTS):
+            queue = nc.sync if q < QUADRANTS - 1 else nc.scalar
             queue.dma_start(
                 out_2[0, 4 * q : 4 * q + 4, :].bitcast(I32),
                 y_scales[32 * q : 32 * q + 4, :].bitcast(I32),

from contextlib import ExitStack

import concourse.mybir as mybir

F32 = mybir.dt.float32
BF16 = mybir.dt.bfloat16
I32 = mybir.dt.int32
U32 = mybir.dt.uint32
U16 = mybir.dt.uint16
U8 = mybir.dt.uint8
FP8X4 = mybir.dt.float8_e4m3fn_x4
ACT = mybir.ActivationFunctionType
MULT = mybir.AluOpType.mult
ADD = mybir.AluOpType.add

P = 128
PACK = 4
QUADRANTS = 4
T = 2048
S = 512
WIDTH = 512
HALF = WIDTH // 2
QUARTER = WIDTH // 4
PER_COLUMN = 16
BANK = 512
CHUNKS = (256, 128, 128)
GATE_TILES = 5
CV_SCALE = 0.0625

FLOPS = 3 * 2 * 512 * 512 * 512


def interleave(copy, grouped, planes):
    copy(
        out=grouped.rearrange("p (c i j) -> p c j i", i=4, j=PACK),
        in_=planes.rearrange("p j (c i) -> p c j i", i=4),
    )


def tile_picked_momprod_none_po_kernel(
    tc, x_words, x_scales, wa, wb, gt, gi, offs, two, fa, fb, out_0, out_1, out_2
):
    nc = tc.nc
    with ExitStack() as ctx:
        keep = ctx.enter_context(tc.tile_pool(name="keep", bufs=1))
        reused = ctx.enter_context(tc.tile_pool(name="reused", bufs=1))
        ring = ctx.enter_context(tc.tile_pool(name="ring", bufs=GATE_TILES))
        psum = ctx.enter_context(tc.psum_pool(name="psum", bufs=1))

        def sbuf(name, shape, dtype):
            return keep.tile(shape, dtype, name=name, align_bytes=64)

        def bank(index):
            return psum.tile([P, BANK], F32, name="bank%d" % index)

        def load_list(name, source):
            tile = keep.tile([P, S // PER_COLUMN], U16, name=name)
            nc.sync.dma_start(tile[:], source)
            return tile

        def load_weight_half(name, w, half):
            tile = sbuf(name, [P, PACK, HALF], F32)
            rows = w.rearrange("(p j) c -> p j c", j=PACK)
            nc.sync.dma_start(tile[:], rows[:, :, half * HALF : (half + 1) * HALF])
            return tile

        def load_place_weights(name, g):
            tile = sbuf(name, [P, PACK], F32)
            nc.sync.dma_start(tile[:], g.rearrange("(p j) o -> p (j o)", j=PACK))
            return tile

        def quantize(codes, scales, grouped):
            nc.vector.quantize_mx(out=codes.bitcast(FP8X4), scales=scales, in_=grouped)

        def product(out, stationary, plane, moving):
            cols = slice(plane * P, (plane + 1) * P)
            nc.tensor.matmul_mx(
                out=out,
                lhsT=stationary[0][:, cols].bitcast(FP8X4),
                lhsT_scale=stationary[1][:, cols],
                rhs=moving[0][:].bitcast(FP8X4),
                rhs_scale=moving[1][:],
                start=True,
                stop=True,
            )

        table_scales = sbuf("table_scales", [P, T], U8)
        nc.vector.memset(table_scales[:].bitcast(I32), 0)
        offs_list = load_list("offs_list", offs)
        two_list = load_list("two_list", two)
        fa_list = load_list("fa_list", fa)
        for q in range(QUADRANTS):
            nc.sync.dma_start(
                table_scales[32 * q : 32 * q + 4, :].bitcast(I32),
                x_scales[0, 4 * q : 4 * q + 4, :].bitcast(I32),
            )
        table_words = sbuf("table_words", [P, T], I32)
        nc.sync.dma_start(table_words[:], x_words[0].rearrange("p c r -> p (c r)").bitcast(I32))
        wa_raw = [load_weight_half("wa_raw%d" % h, wa, h) for h in range(2)]
        wb_raw = [load_weight_half("wb_raw%d" % h, wb, h) for h in range(2)]
        gt_places = load_place_weights("gt_places", gt)
        gi_places = load_place_weights("gi_places", gi)
        fb_list = load_list("fb_list", fb)

        a_rows = [sbuf("a_rows%d" % j, [P, 2 * WIDTH], F32) for j in range(PACK)]
        b_rows = [sbuf("b_rows%d" % j, [P, WIDTH], F32) for j in range(PACK)]
        for rows in a_rows:
            nc.vector.memset(rows[:, WIDTH:], 0.0)

        warm = sbuf("warm", [P, 1], F32)
        nc.scalar.activation(warm[:], a_rows[0][:, WIDTH : WIDTH + 1], ACT.Sigmoid)

        def pick_scales(name, token_list):
            listed = sbuf(name + "_listed", [P, S], U8)
            nc.vector.tensor_copy(listed[:], table_scales[:].indirect(token_list[:]))
            dealt = sbuf(name, [P, S], U8)
            nc.vector.tensor_copy(
                dealt[:].rearrange("p (j m) -> p j m", j=PACK),
                listed[:].rearrange("p (m j) -> p j m", j=PACK),
            )
            return dealt

        def pick_words(dealt, token_list):
            nc.vector.tensor_copy(
                dealt[:].rearrange("p (j m) -> p m j", j=PACK),
                table_words[:].bitcast(U32).indirect(token_list[:]),
            )
            return dealt

        xa_scales = pick_scales("xa_scales", offs_list)
        xb_scales = pick_scales("xb_scales", two_list)
        xa = (pick_words(sbuf("xa_words", [P, S], U32), offs_list), xa_scales)

        wa_q = (sbuf("wa_codes", [P, WIDTH], U32), sbuf("wa_scales", [P, WIDTH], U8))
        wa_grouped = reused.tile([P, PACK * WIDTH], BF16, name="wa_grouped", align_bytes=64, offset=0)
        split = PACK * (HALF + QUARTER)
        interleave(nc.scalar.copy, wa_grouped[:, : PACK * HALF], wa_raw[0][:])
        interleave(nc.scalar.copy, wa_grouped[:, PACK * HALF : split], wa_raw[1][:, :, :QUARTER])
        interleave(nc.vector.tensor_copy, wa_grouped[:, split:], wa_raw[1][:, :, QUARTER:])
        a_banks = [bank(j) for j in range(PACK)]
        for h in range(2):
            cols = slice(h * HALF, (h + 1) * HALF)
            quantize(wa_q[0][:, cols], wa_q[1][:, cols], wa_grouped[:, PACK * cols.start : PACK * cols.stop])
        for j in range(PACK):
            product(a_banks[j][:], xa, j, wa_q)

        xb_words = reused.tile([P, S], U32, name="xb_words", align_bytes=64, offset=0)
        xb = (pick_words(xb_words, two_list), xb_scales)

        wb_grouped = sbuf("wb_grouped", [P, PACK * WIDTH], BF16)
        interleave(nc.scalar.copy, wb_grouped[:, : PACK * HALF], wb_raw[0][:])
        nc.gpsimd.tensor_scalar(
            wb_grouped[:, PACK * HALF :].rearrange("p (c j) -> p c j", j=PACK),
            wb_raw[1][:].rearrange("p j c -> p c j"),
            1.0,
            0.0,
            MULT,
            ADD,
        )

        def gate(out, rows, feature_list, cols):
            offsets = feature_list[:, cols.start // PER_COLUMN : cols.stop // PER_COLUMN]
            nc.scalar.activation(out, rows[:].indirect(offsets), ACT.Sigmoid)

        def weigh(out, sums, places, j, gates):
            nc.vector.scalar_tensor_tensor(out, sums, places[:, j : j + 1], gates, MULT, MULT)

        a_gates = [sbuf("a_gates%d" % j, [P, WIDTH], F32) for j in range(PACK)]

        def gate_a(j):
            copy = nc.scalar.copy if j == 0 else nc.vector.tensor_copy
            copy(a_rows[j][:, :WIDTH], a_banks[j][:])
            gate(a_gates[j][:], a_rows[j], fa_list, slice(0, WIDTH))

        wb_q = (sbuf("wb_codes", [P, WIDTH], U32), sbuf("wb_scales", [P, WIDTH], U8))
        b_banks = [bank(PACK + j) for j in range(PACK)]
        z_planes = sbuf("z_planes", [P, PACK, WIDTH], BF16)

        for j in range(PACK - 1):
            gate_a(j)
        quantize(wb_q[0][:], wb_q[1][:], wb_grouped[:])
        for j in range(PACK):
            product(b_banks[j][:], xb, j, wb_q)
        gate_a(PACK - 1)
        weigh(z_planes[:, 0, :], a_banks[0][:], gt_places, 0, a_gates[0][:])
        for j in range(1, PACK):
            weigh(z_planes[:, j, :], a_banks[j][:], gt_places, j, a_gates[j][:])
            nc.vector.tensor_copy(b_rows[j - 1][:], b_banks[j - 1][:])
        nc.vector.tensor_copy(b_rows[PACK - 1][:], b_banks[PACK - 1][:])

        z_grouped = sbuf("z_grouped", [P, PACK * WIDTH], BF16)
        nc.vector.tensor_copy(
            z_grouped[:].rearrange("p (u m i j) -> p m u i j", u=PACK, i=2, j=PACK),
            z_planes[:].rearrange("p j (m i u) -> p m u i j", u=PACK, i=2),
        )
        z_q = (sbuf("z_codes", [P, WIDTH], U32), sbuf("z_scales", [P, WIDTH], U8))
        quantize(z_q[0][:], z_q[1][:], z_grouped[:])

        chunk_cols = [slice(sum(CHUNKS[:c]), sum(CHUNKS[: c + 1])) for c in range(len(CHUNKS))]
        last = len(CHUNKS) - 1
        out_rows = out_0.rearrange("(p u) c -> p u c", u=PACK)
        out_words = out_1[0].rearrange("p c r -> p (c r)").bitcast(I32)
        y_scales = sbuf("y_scales", [P, WIDTH], U8)
        filled = []
        for c, width in enumerate(CHUNKS):
            z2_planes = sbuf("z2_planes%d" % c, [P, PACK, width], BF16)
            for j in range(PACK):
                gates = ring.tile([P, width], F32, name="b_gates")
                gate(gates[:], b_rows[j], fb_list, chunk_cols[c])
                weigh(z2_planes[:, j, :], b_banks[j][:, chunk_cols[c]], gi_places, j, gates[:])
            z2_grouped = sbuf("z2_grouped%d" % c, [P, PACK * width], BF16)
            interleave(nc.vector.tensor_copy, z2_grouped[:], z2_planes[:])
            z2_q = (sbuf("z2_codes%d" % c, [P, width], U32), sbuf("z2_scales%d" % c, [P, width], U8))
            quantize(z2_q[0][:], z2_q[1][:], z2_grouped[:])
            per_bank = BANK // width
            for first in range(0, PACK, per_bank):
                sums = bank(len(filled))
                for k in range(per_bank):
                    product(sums[:, k * width : (k + 1) * width], z_q, first + k, z2_q)
                filled.append((c, first, sums))

        ys = [sbuf("y%d" % c, [P, PACK * width], F32) for c, width in enumerate(CHUNKS)]
        for c, first, sums in filled:
            width = CHUNKS[c]
            if c == last:
                last_grouped = sbuf("y_grouped%d" % c, [P, PACK * width], BF16)
                nc.scalar.activation(
                    last_grouped[:].rearrange("p (c u) -> p c u", u=PACK),
                    sums[:].rearrange("p (u c) -> p c u", u=PACK),
                    ACT.Tanh,
                    scale=CV_SCALE,
                )
            part = ys[c][:, first * width : first * width + BANK]
            nc.scalar.activation(part, sums[:], ACT.Tanh, scale=CV_SCALE)
            nc.sync.dma_start(
                out_rows[:, first : first + BANK // width, chunk_cols[c]],
                part.rearrange("p (u c) -> p u c", c=width),
            )

        y_codes = sbuf("y_codes", [P, WIDTH], U32)
        for c in range(last):
            y_grouped = sbuf("y_grouped%d" % c, [P, PACK * CHUNKS[c]], BF16)
            interleave(nc.vector.tensor_copy, y_grouped[:], ys[c][:].rearrange("p (u c) -> p u c", u=PACK))
            quantize(y_codes[:, chunk_cols[c]], y_scales[:, chunk_cols[c]], y_grouped[:])
        early = slice(0, chunk_cols[last].start)
        late = chunk_cols[last]
        nc.sync.dma_start(out_words[:, early], y_codes[:, early].bitcast(I32))
        quantize(y_codes[:, late], y_scales[:, late], last_grouped[:])
        nc.scalar.dma_start(out_words[:, late], y_codes[:, late].bitcast(I32))
        for q in range(QUADRANTS):
            queue = nc.sync if q < QUADRANTS - 1 else nc.scalar
            queue.dma_start(
                out_2[0, 4 * q : 4 * q + 4, :].bitcast(I32),
                y_scales[32 * q : 32 * q + 4, :].bitcast(I32),
            )
